import numpy as np
import ml_dtypes


def mxq(x, axis, fmt="e4m3"):
    dtype, down = {"e4m3": (ml_dtypes.float8_e4m3fn, 7), "e5m2": (ml_dtypes.float8_e5m2, 14)}[fmt]
    v = np.moveaxis(np.asarray(x, np.float32).astype(ml_dtypes.bfloat16).astype(np.float64), axis, -1)
    blocks = v.reshape(v.shape[:-1] + (-1, 32))
    amax = np.abs(blocks).max(-1, keepdims=True)
    byte = np.maximum(np.where(amax > 0, np.frexp(amax)[1] - 1 + 127, 0) - down, 1)
    scale = np.exp2(byte - 127.0)
    codes = (blocks / scale).astype(np.float32).astype(dtype).astype(np.float64)
    return np.moveaxis((codes * scale).reshape(v.shape), -1, axis)


WIDE = False


def mx_kscale(k):
    if not WIDE:
        return np.ones(k)
    levels = np.array([10, -10, 5, -5, 0])
    if k % 512:
        return np.exp2(np.random.permutation(np.resize(levels, k // 32))).repeat(32)
    a = np.empty((k // 512, 16))
    for p in range(k // 512):
        a[p, :8] = np.random.permutation(np.resize(levels, 8))
        for g in range(8):
            far = levels[np.abs(levels - a[p, g]) >= 10]
            a[p, g + 8] = far[np.random.randint(len(far))]
    return np.exp2(a.ravel()).repeat(32)


def f64(x):
    return np.asarray(x).astype(np.float64)


def striped8(idx):
    return np.asarray(idx).reshape(8, -1, 16).transpose(0, 2, 1).reshape(128, -1).astype(np.uint16)


def unstriped8(offs):
    return offs.reshape(8, 16, -1).transpose(0, 2, 1).reshape(8, -1).astype(np.int64)


def pick8(x, idx, run):
    r = np.arange(len(x))
    return x[r[:, None], idx[r % (8 * run) // run]]


E2M1 = np.array([0.0, 0.5, 1.0, 1.5, 2.0, 3.0, 4.0, 6.0, -0.0, -0.5, -1.0, -1.5, -2.0, -3.0, -4.0, -6.0])


def pack_weight(w, fmt):
    k, n = w.shape
    w = f64(np.asarray(w, np.float32).astype(ml_dtypes.bfloat16)).reshape(k // 32, 32, n)
    amax = np.abs(w).max(1)
    if fmt == "e4m3":
        byte = np.frexp(amax)[1] - 1 + 127 - 7
    else:
        mant, ex = np.frexp(amax / 6.0)
        byte = np.where(mant > 0.5, ex, ex - 1) + 127
    byte = np.clip(np.where(amax > 0, byte, 1), 1, 254)
    scaled = (w * np.exp2(127.0 - byte)[:, None, :]).reshape(k, n).astype(np.float32)
    by_word = np.ascontiguousarray(scaled.reshape(k // 512, 128, 4, n).transpose(0, 1, 3, 2))
    if fmt == "e4m3":
        words = by_word.astype(ml_dtypes.float8_e4m3fn).view(np.uint8)
    else:
        c = by_word.astype(ml_dtypes.float4_e2m1fn).view(np.uint8) & 0xF
        words = (c[..., 0::2] | (c[..., 1::2] << 4)).reshape(k // 512, 128, 2 * n)
    return np.ascontiguousarray(words), np.ascontiguousarray(byte.astype(np.uint8).reshape(k // 512, 16, n))


def unpack_weight(words, scales, fmt):
    g, _, n = scales.shape
    words = np.ascontiguousarray(words).reshape(g, 128, n, -1)
    if fmt == "e4m3":
        vals = words.view(ml_dtypes.float8_e4m3fn).astype(np.float64)
    else:
        nib = np.empty((g, 128, n, 4), np.uint8)
        nib[..., 0::2] = words & 0xF
        nib[..., 1::2] = words >> 4
        vals = E2M1[nib]
    vals = vals * np.repeat(np.exp2(scales.astype(np.float64) - 127.0), 8, axis=1)[..., None]
    return vals.transpose(0, 1, 3, 2).reshape(g * 512, n)


def softplus(v):
    return np.log(1.0 + np.exp(v))


D, T, I, Q = 512, 1024, 512, 128


def setup_inputs():
    n = np.random.standard_normal
    idx = np.stack([np.random.permutation(T)[:I] for _ in range(8)])
    idx2 = np.stack([np.random.permutation(T)[:I] for _ in range(8)])
    idx3 = np.stack([np.random.permutation(T)[:I] for _ in range(8)])
    fd = mx_kscale(D)
    keysp = pack_weight(n((D, T)) / fd[:, None], "e4m3")
    return {
        "query": (n((D, Q)) * 0.9 / np.sqrt(D) * fd[:, None]).astype(np.float32),
        "query2": (n((D, Q)) * 0.9 / np.sqrt(D) * fd[:, None]).astype(np.float32),
        "keys_words": keysp[0],
        "keys_scales": keysp[1],
        "lam": (np.random.uniform(0.6, 1.2, (Q, 1))).astype(np.float32),
        "old": (1.0 * n((Q, T))).astype(np.float32),
        "share2": (np.random.uniform(0.4, 1.2, (Q, 1))).astype(np.float32),
        "offs": striped8(idx),
        "offs2": striped8(idx2),
        "offs3": striped8(idx3),
    }


def reference(query, query2, keys_words, keys_scales, lam, old, share2, offs, offs2, offs3):
    idx = unstriped8(offs)
    idx2 = unstriped8(offs2)
    idx3 = unstriped8(offs3)
    keysu = unpack_weight(keys_words, keys_scales, "e4m3")
    queryq = mxq(f64(query), 0, "e4m3")
    a = queryq.T @ keysu
    query2q = mxq(f64(query2), 0, "e4m3")
    b = query2q.T @ keysu
    w = pick8(a, idx, 16) / (softplus(pick8(b, idx2, 16)) + 0.5) * f64(lam)
    f1 = np.zeros((Q, T))
    f1[np.arange(Q)[:, None], idx[np.arange(Q) % 128 // 16]] = w
    f2 = np.zeros((Q, T))
    f2[np.arange(Q)[:, None], idx3[np.arange(Q) % 128 // 16]] = w
    y = f64(old) + f1 + f2 * f64(share2)
    return y

@@ -1,0 +1,186 @@
+import math
+from contextlib import ExitStack
+
+import concourse.mybir as mybir
+from concourse.masks import make_identity
+
+D, T, I, Q = 512, 1024, 512, 128
+FLOPS = 2 * 2 * D * Q * T
+
+F32 = mybir.dt.float32
+BF16 = mybir.dt.bfloat16
+I32 = mybir.dt.int32
+U32 = mybir.dt.uint32
+U16 = mybir.dt.uint16
+U8 = mybir.dt.uint8
+FP8X4 = mybir.dt.float8_e4m3fn_x4
+ALU = mybir.AluOpType
+ACT = mybir.ActivationFunctionType
+
+P = 128
+PACK = 4
+BANK = 512
+B_PASS = 256
+PER_COLUMN = 16
+EXP_CAP = 40.0
+SPLIT = 192
+BY_SCALAR = 384
+
+
+def offsets(lists, slots):
+    return lists[:, slots.start // PER_COLUMN : slots.stop // PER_COLUMN]
+
+
+def tile_attend_worthfor_lean_twiceput_heads_kernel(
+    tc, query, query2, keys_words, keys_scales, lam, old, share2, offs, offs2, offs3, out
+):
+    nc = tc.nc
+    with ExitStack() as ctx:
+        sb = ctx.enter_context(tc.tile_pool(name="sb", bufs=1))
+        ps = ctx.enter_context(tc.psum_pool(name="ps", bufs=1))
+
+        k_scale = sb.tile([P, T], U8, name="k_scale", align_bytes=64)
+        nc.vector.memset(k_scale[:].bitcast(I32), 0)
+        lam_sb = sb.tile([P, 1], F32, name="lam_sb")
+        nc.gpsimd.dma_start(out=lam_sb[:], in_=lam)
+        q2_raw = sb.tile([P, PACK, Q], F32, name="q2_raw")
+        nc.sync.dma_start(out=q2_raw[:], in_=query2.rearrange("(p j) q -> p j q", j=PACK))
+        for quad in range(4):
+            nc.sync.dma_start(
+                out=k_scale[32 * quad : 32 * quad + 4, :].bitcast(I32),
+                in_=keys_scales[0, 4 * quad : 4 * quad + 4, :].bitcast(I32),
+            )
+        words = keys_words[0].rearrange("p n t -> p (n t)")
+        k_words = []
+        for h in range(2):
+            kw = sb.tile([P, BANK], U32, name="k_words%d" % h, align_bytes=64)
+            nc.sync.dma_start(
+                out=kw[:].bitcast(I32),
+                in_=words[:, PACK * BANK * h : PACK * BANK * (h + 1)].bitcast(I32),
+            )
+            k_words.append(kw)
+        q_raw = sb.tile([P, PACK, Q], F32, name="q_raw")
+        nc.sync.dma_start(out=q_raw[:], in_=query.rearrange("(p j) q -> p j q", j=PACK))
+        list2 = sb.tile([P, I // PER_COLUMN], U16, name="list2")
+        nc.sync.dma_start(list2[:], offs2)
+        list1 = sb.tile([P, I // PER_COLUMN], U16, name="list1")
+        nc.sync.dma_start(list1[:], offs)
+        list3 = sb.tile([P, I // PER_COLUMN], U16, name="list3")
+        nc.sync.dma_start(list3[:], offs3)
+        old_sb = sb.tile([P, T], F32, name="old_sb")
+        nc.sync.dma_start(out=old_sb[:], in_=old)
+        share_sb = sb.tile([P, 1], F32, name="share_sb")
+        nc.gpsimd.dma_start(out=share_sb[:], in_=share2)
+
+        f1 = sb.tile([P, T], F32, name="f1")
+        f2 = sb.tile([P, T], F32, name="f2")
+        nc.vector.memset(f1[:], 0.0)
+        nc.vector.memset(f2[:], 0.0)
+        ident = sb.tile([P, P], F32, name="ident")
+        make_identity(nc, ident[:])
+
+        lam_row = sb.tile([P, I], F32, name="lam_row")
+        nc.scalar.copy(out=lam_row[:], in_=lam_sb[:].to_broadcast([P, I]))
+
+        def quantise(raw, name, cast):
+            grouped = sb.tile([P, Q, PACK], BF16, name=name + "_bf", align_bytes=64)
+            cast(out=grouped[:], in_=raw[:].rearrange("p j q -> p q j"))
+            codes = sb.tile([P, Q], U32, name=name + "_codes", align_bytes=64)
+            scales = sb.tile([P, Q], U8, name=name + "_scales", align_bytes=64)
+            nc.vector.quantize_mx(
+                out=codes[:].bitcast(FP8X4),
+                scales=scales[:],
+                in_=grouped[:].rearrange("p q j -> p (q j)"),
+            )
+            return codes, scales
+
+        def score(codes, scales, first, width, tag):
+            h, within = divmod(first, BANK)
+            bank = ps.tile([P, width], F32, name=tag, tag=tag)
+            nc.tensor.matmul_mx(
+                out=bank[:],
+                lhsT=codes[:].bitcast(FP8X4),
+                lhsT_scale=scales[:],
+                rhs=k_words[h][:, within : within + width].bitcast(FP8X4),
+                rhs_scale=k_scale[:, first : first + width],
+                start=True,
+                stop=True,
+            )
+            return bank
+
+        q2_codes, q2_scales = quantise(q2_raw, "q2", nc.vector.tensor_copy)
+        q_codes, q_scales = quantise(q_raw, "q", nc.scalar.copy)
+        b_banks = [score(q2_codes, q2_scales, B_PASS * n, B_PASS, "bank%d" % n) for n in range(T // B_PASS)]
+        a_banks = [score(q_codes, q_scales, BANK * h, BANK, "a_bank%d" % h) for h in range(2)]
+
+        b_sb = sb.tile([P, T], F32, name="b_sb")
+        for n, bank in enumerate(b_banks):
+            copy_out = nc.scalar.copy if n % 2 == 0 else nc.vector.tensor_copy
+            copy_out(out=b_sb[:, B_PASS * n : B_PASS * (n + 1)], in_=bank[:])
+
+        a_sb = sb.tile([P, T], F32, name="a_sb")
+        nc.scalar.copy(out=a_sb[:, :BANK], in_=a_banks[0][:])
+
+        x = sb.tile([P, I], F32, name="x")
+        x_cap = sb.tile([P, I], F32, name="x_cap")
+        e = sb.tile([P, I], F32, name="e")
+        halves = [slice(0, I // 2), slice(I // 2, I)]
+        for s in halves:
+            nc.vector.tensor_copy(x[:, s], b_sb[:].indirect(offsets(list2, s)))
+            nc.vector.tensor_scalar(out=x_cap[:, s], in0=x[:, s], scalar1=EXP_CAP, scalar2=None, op0=ALU.min)
+            nc.scalar.activation(out=e[:, s], in_=x_cap[:, s], func=ACT.Exp)
+
+        nc.vector.tensor_copy(out=a_sb[:, BANK:], in_=a_banks[1][:])
+        a_lam = sb.tile([P, I], F32, name="a_lam")
+        nc.vector.tensor_tensor(a_lam[:], a_sb[:].indirect(list1[:]), lam_row[:], ALU.mult)
+
+        root_e = math.exp(0.5)
+        soft = sb.tile([P, I], F32, name="soft")
+        den = sb.tile([P, I], F32, name="den")
+        log_den = sb.tile([P, BY_SCALAR], F32, name="log_den")
+        inv = sb.tile([P, I], F32, name="inv")
+        for s in (slice(0, SPLIT), slice(SPLIT, I)):
+            nc.scalar.activation(out=soft[:, s], in_=e[:, s], func=ACT.Ln, scale=root_e, bias=root_e)
+            nc.vector.scalar_tensor_tensor(
+                out=den[:, s], in0=x[:, s], scalar=0.5, in1=soft[:, s], op0=ALU.add, op1=ALU.max
+            )
+        for s in (slice(0, SPLIT), slice(SPLIT, BY_SCALAR)):
+            nc.scalar.activation(out=log_den[:, s], in_=den[:, s], func=ACT.Ln)
+        by_vector = slice(BY_SCALAR, I)
+        by_scalar = slice(0, BY_SCALAR)
+        nc.vector.reciprocal(out=inv[:, by_vector], in_=den[:, by_vector])
+        nc.scalar.activation(out=inv[:, by_scalar], in_=log_den[:], func=ACT.Exp, scale=-1.0)
+
+        blocks = BANK // P
+        turned_banks = [ps.tile([P, blocks, P], F32, name="turned%d" % h) for h in range(2)]
+        for h in range(2):
+            for j in range(blocks):
+                c = slice(BANK * h + P * j, BANK * h + P * (j + 1))
+                nc.tensor.matmul(turned_banks[h][:, j, :], old_sb[:, c], ident[:], start=(j == 0), stop=False, is_transpose=True)
+
+        for s in (by_vector, by_scalar):
+            nc.vector.tensor_tensor(f1[:].indirect(offsets(list1, s)), a_lam[:, s], inv[:, s], ALU.mult)
+            nc.vector.tensor_tensor(f2[:].indirect(offsets(list3, s)), a_lam[:, s], inv[:, s], ALU.mult)
+
+        for h in range(2):
+            for j in range(blocks):
+                c = slice(BANK * h + P * j, BANK * h + P * (j + 1))
+                nc.tensor.matmul(turned_banks[h][:, j, :], f1[:, c], ident[:], start=False, stop=(j == blocks - 1), is_transpose=True)
+        for h in range(2):
+            turned = sb.tile([P, blocks, P], F32, name="turned_sb%d" % h)
+            nc.scalar.copy(out=turned[:], in_=turned_banks[h][:])
+            back = ps.tile([P, blocks, P], F32, name="back%d" % h, tag="bank%d" % h)
+            for j in range(blocks):
+                nc.tensor.transpose(back[:, j, :], turned[:, j, :], ident[:])
+            cols = slice(BANK * h, BANK * (h + 1))
+            result = sb.tile([P, BANK], F32, name="result%d" % h)
+            nc.vector.scalar_tensor_tensor(
+                out=result[:],
+                in0=f2[:, cols],
+                scalar=share_sb[:],
+                in1=back[:].rearrange("p j c -> p (j c)"),
+                op0=ALU.mult,
+                op1=ALU.add,
+            )
+            queue = nc.sync if h == 0 else nc.scalar
+            queue.dma_start(out=out[:, cols], in_=result[:])

@@ -21,10 +21,11 @@ P = 128
 PACK = 4
 BANK = 512
 B_PASS = 256
+B_PASSES = (256, 256, 256, 128, 128)
 PER_COLUMN = 16
 EXP_CAP = 40.0
-SPLIT = 192
-BY_SCALAR = 384
+SPLIT = 320
+BY_VECTOR = 128
 
 
 def offsets(lists, slots):
@@ -40,11 +41,11 @@ def tile_attend_worthfor_lean_twiceput_heads_kernel(
         ps = ctx.enter_context(tc.psum_pool(name="ps", bufs=1))
 
         k_scale = sb.tile([P, T], U8, name="k_scale", align_bytes=64)
-        nc.vector.memset(k_scale[:].bitcast(I32), 0)
-        lam_sb = sb.tile([P, 1], F32, name="lam_sb")
-        nc.gpsimd.dma_start(out=lam_sb[:], in_=lam)
+        nc.gpsimd.memset(k_scale[:].bitcast(I32), 0)
         q2_raw = sb.tile([P, PACK, Q], F32, name="q2_raw")
         nc.sync.dma_start(out=q2_raw[:], in_=query2.rearrange("(p j) q -> p j q", j=PACK))
+        q_raw = sb.tile([P, PACK, Q], F32, name="q_raw")
+        nc.sync.dma_start(out=q_raw[:], in_=query.rearrange("(p j) q -> p j q", j=PACK))
         for quad in range(4):
             nc.sync.dma_start(
                 out=k_scale[32 * quad : 32 * quad + 4, :].bitcast(I32),
@@ -53,34 +54,29 @@ def tile_attend_worthfor_lean_twiceput_heads_kernel(
         words = keys_words[0].rearrange("p n t -> p (n t)")
         k_words = []
         for h in range(2):
-            kw = sb.tile([P, BANK], U32, name="k_words%d" % h, align_bytes=64)
+            kw = sb.tile([P, BANK], U32, name="k_words%d" % h, tag="words%d" % h, align_bytes=64)
             nc.sync.dma_start(
                 out=kw[:].bitcast(I32),
                 in_=words[:, PACK * BANK * h : PACK * BANK * (h + 1)].bitcast(I32),
             )
             k_words.append(kw)
-        q_raw = sb.tile([P, PACK, Q], F32, name="q_raw")
-        nc.sync.dma_start(out=q_raw[:], in_=query.rearrange("(p j) q -> p j q", j=PACK))
         list2 = sb.tile([P, I // PER_COLUMN], U16, name="list2")
         nc.sync.dma_start(list2[:], offs2)
         list1 = sb.tile([P, I // PER_COLUMN], U16, name="list1")
         nc.sync.dma_start(list1[:], offs)
+        lam_sb = sb.tile([P, 1], F32, name="lam_sb")
+        nc.sync.dma_start(out=lam_sb[:], in_=lam)
         list3 = sb.tile([P, I // PER_COLUMN], U16, name="list3")
         nc.sync.dma_start(list3[:], offs3)
         old_sb = sb.tile([P, T], F32, name="old_sb")
         nc.sync.dma_start(out=old_sb[:], in_=old)
         share_sb = sb.tile([P, 1], F32, name="share_sb")
-        nc.gpsimd.dma_start(out=share_sb[:], in_=share2)
+        nc.sync.dma_start(out=share_sb[:], in_=share2)
 
         f1 = sb.tile([P, T], F32, name="f1")
         f2 = sb.tile([P, T], F32, name="f2")
         nc.vector.memset(f1[:], 0.0)
         nc.vector.memset(f2[:], 0.0)
-        ident = sb.tile([P, P], F32, name="ident")
-        make_identity(nc, ident[:])
-
-        lam_row = sb.tile([P, I], F32, name="lam_row")
-        nc.scalar.copy(out=lam_row[:], in_=lam_sb[:].to_broadcast([P, I]))
 
         def quantise(raw, name, cast):
             grouped = sb.tile([P, Q, PACK], BF16, name=name + "_bf", align_bytes=64)
@@ -94,11 +90,10 @@ def tile_attend_worthfor_lean_twiceput_heads_kernel(
             )
             return codes, scales
 
-        def score(codes, scales, first, width, tag):
+        def score(bank, codes, scales, first, width):
             h, within = divmod(first, BANK)
-            bank = ps.tile([P, width], F32, name=tag, tag=tag)
             nc.tensor.matmul_mx(
-                out=bank[:],
+                out=bank,
                 lhsT=codes[:].bitcast(FP8X4),
                 lhsT_scale=scales[:],
                 rhs=k_words[h][:, within : within + width].bitcast(FP8X4),
@@ -106,79 +101,90 @@ def tile_attend_worthfor_lean_twiceput_heads_kernel(
                 start=True,
                 stop=True,
             )
-            return bank
 
         q2_codes, q2_scales = quantise(q2_raw, "q2", nc.vector.tensor_copy)
         q_codes, q_scales = quantise(q_raw, "q", nc.scalar.copy)
-        b_banks = [score(q2_codes, q2_scales, B_PASS * n, B_PASS, "bank%d" % n) for n in range(T // B_PASS)]
-        a_banks = [score(q_codes, q_scales, BANK * h, BANK, "a_bank%d" % h) for h in range(2)]
-
         b_sb = sb.tile([P, T], F32, name="b_sb")
-        for n, bank in enumerate(b_banks):
-            copy_out = nc.scalar.copy if n % 2 == 0 else nc.vector.tensor_copy
-            copy_out(out=b_sb[:, B_PASS * n : B_PASS * (n + 1)], in_=bank[:])
-
-        a_sb = sb.tile([P, T], F32, name="a_sb")
-        nc.scalar.copy(out=a_sb[:, :BANK], in_=a_banks[0][:])
+        first = 0
+        for n, width in enumerate(B_PASSES):
+            bank = ps.tile([P, width], F32, name="b_bank%d" % n, tag="bank%d" % n)
+            score(bank[:], q2_codes, q2_scales, first, width)
+            copy_out = nc.vector.tensor_copy if n % 2 == 0 else nc.scalar.copy
+            copy_out(out=b_sb[:, first : first + width], in_=bank[:])
+            first = first + width
 
         x = sb.tile([P, I], F32, name="x")
         x_cap = sb.tile([P, I], F32, name="x_cap")
         e = sb.tile([P, I], F32, name="e")
         halves = [slice(0, I // 2), slice(I // 2, I)]
+        nc.vector.tensor_copy(x[:, halves[0]], b_sb[:].indirect(offsets(list2, halves[0])))
+        nc.scalar.activation(x[:, halves[1]], b_sb[:].indirect(offsets(list2, halves[1])), ACT.Copy)
         for s in halves:
-            nc.vector.tensor_copy(x[:, s], b_sb[:].indirect(offsets(list2, s)))
             nc.vector.tensor_scalar(out=x_cap[:, s], in0=x[:, s], scalar1=EXP_CAP, scalar2=None, op0=ALU.min)
             nc.scalar.activation(out=e[:, s], in_=x_cap[:, s], func=ACT.Exp)
 
-        nc.vector.tensor_copy(out=a_sb[:, BANK:], in_=a_banks[1][:])
+        a_sb = sb.tile([P, T], F32, name="a_sb")
+        for h in range(2):
+            cols = slice(BANK * h, BANK * (h + 1))
+            bank = ps.tile([P, BANK], F32, name="a_bank%d" % h, tag="bank%d" % (3 + h))
+            score(bank[:], q_codes, q_scales, BANK * h, BANK)
+            nc.vector.tensor_copy(out=a_sb[:, cols], in_=bank[:])
         a_lam = sb.tile([P, I], F32, name="a_lam")
-        nc.vector.tensor_tensor(a_lam[:], a_sb[:].indirect(list1[:]), lam_row[:], ALU.mult)
+        a_picked = sb.tile([P, I], F32, name="a_picked", tag="picked_then_den")
+        nc.vector.tensor_copy(a_picked[:], a_sb[:].indirect(list1[:]))
+        nc.vector.tensor_scalar(out=a_lam[:], in0=a_picked[:], scalar1=lam_sb[:], scalar2=None, op0=ALU.mult)
 
         root_e = math.exp(0.5)
         soft = sb.tile([P, I], F32, name="soft")
-        den = sb.tile([P, I], F32, name="den")
-        log_den = sb.tile([P, BY_SCALAR], F32, name="log_den")
+        den = sb.tile([P, I], F32, name="den", tag="picked_then_den")
+        log_den = sb.tile([P, I], F32, name="log_den")
         inv = sb.tile([P, I], F32, name="inv")
-        for s in (slice(0, SPLIT), slice(SPLIT, I)):
+        for s in (slice(SPLIT, I), slice(0, SPLIT)):
             nc.scalar.activation(out=soft[:, s], in_=e[:, s], func=ACT.Ln, scale=root_e, bias=root_e)
             nc.vector.scalar_tensor_tensor(
                 out=den[:, s], in0=x[:, s], scalar=0.5, in1=soft[:, s], op0=ALU.add, op1=ALU.max
             )
-        for s in (slice(0, SPLIT), slice(SPLIT, BY_SCALAR)):
+        for s in (slice(SPLIT, I), slice(BY_VECTOR, SPLIT)):
             nc.scalar.activation(out=log_den[:, s], in_=den[:, s], func=ACT.Ln)
-        by_vector = slice(BY_SCALAR, I)
-        by_scalar = slice(0, BY_SCALAR)
+        by_vector = slice(0, BY_VECTOR)
+        by_scalar = slice(BY_VECTOR, I)
         nc.vector.reciprocal(out=inv[:, by_vector], in_=den[:, by_vector])
-        nc.scalar.activation(out=inv[:, by_scalar], in_=log_den[:], func=ACT.Exp, scale=-1.0)
+        nc.scalar.activation(out=inv[:, by_scalar], in_=log_den[:, by_scalar], func=ACT.Exp, scale=-1.0)
 
         blocks = BANK // P
-        turned_banks = [ps.tile([P, blocks, P], F32, name="turned%d" % h) for h in range(2)]
-        for h in range(2):
-            for j in range(blocks):
-                c = slice(BANK * h + P * j, BANK * h + P * (j + 1))
-                nc.tensor.matmul(turned_banks[h][:, j, :], old_sb[:, c], ident[:], start=(j == 0), stop=False, is_transpose=True)
+        ident = sb.tile([P, P], F32, name="ident", tag="words1", align_bytes=64)
+        make_identity(nc, ident[:])
+        quarters = T // B_PASS
+        pair = B_PASS // P
+        tags = ["bank0", "bank1", "bank2", "bank5"]
+        turned_banks = [ps.tile([P, pair, P], F32, name="turned%d" % n, tag=tags[n]) for n in range(quarters)]
+        for n in range(quarters):
+            for j in range(pair):
+                c = slice(B_PASS * n + P * j, B_PASS * n + P * (j + 1))
+                nc.tensor.matmul(turned_banks[n][:, j, :], old_sb[:, c], ident[:], start=(j == 0), stop=False, is_transpose=True)
 
         for s in (by_vector, by_scalar):
             nc.vector.tensor_tensor(f1[:].indirect(offsets(list1, s)), a_lam[:, s], inv[:, s], ALU.mult)
             nc.vector.tensor_tensor(f2[:].indirect(offsets(list3, s)), a_lam[:, s], inv[:, s], ALU.mult)
 
+        back = [ps.tile([P, BANK], F32, name="back%d" % h, tag="bank%d" % (3 + h)) for h in range(2)]
+        for n in range(quarters):
+            for j in range(pair):
+                c = slice(B_PASS * n + P * j, B_PASS * n + P * (j + 1))
+                nc.tensor.matmul(turned_banks[n][:, j, :], f1[:, c], ident[:], start=False, stop=(j == pair - 1), is_transpose=True)
+            turned = sb.tile([P, pair, P], F32, name="turned_sb%d" % n)
+            nc.scalar.copy(out=turned[:], in_=turned_banks[n][:])
+            for j in range(pair):
+                h, within = divmod(B_PASS * n + P * j, BANK)
+                nc.tensor.transpose(back[h][:, within : within + P], turned[:, j, :], ident[:])
         for h in range(2):
-            for j in range(blocks):
-                c = slice(BANK * h + P * j, BANK * h + P * (j + 1))
-                nc.tensor.matmul(turned_banks[h][:, j, :], f1[:, c], ident[:], start=False, stop=(j == blocks - 1), is_transpose=True)
-        for h in range(2):
-            turned = sb.tile([P, blocks, P], F32, name="turned_sb%d" % h)
-            nc.scalar.copy(out=turned[:], in_=turned_banks[h][:])
-            back = ps.tile([P, blocks, P], F32, name="back%d" % h, tag="bank%d" % h)
-            for j in range(blocks):
-                nc.tensor.transpose(back[:, j, :], turned[:, j, :], ident[:])
             cols = slice(BANK * h, BANK * (h + 1))
             result = sb.tile([P, BANK], F32, name="result%d" % h)
             nc.vector.scalar_tensor_tensor(
                 out=result[:],
                 in0=f2[:, cols],
                 scalar=share_sb[:],
-                in1=back[:].rearrange("p j c -> p (j c)"),
+                in1=back[h][:],
                 op0=ALU.mult,
                 op1=ALU.add,
             )

@@ -123,20 +123,19 @@ def tile_attend_worthfor_lean_twiceput_heads_kernel(
             nc.vector.tensor_scalar(out=x_cap[:, s], in0=x[:, s], scalar1=EXP_CAP, scalar2=None, op0=ALU.min)
             nc.scalar.activation(out=e[:, s], in_=x_cap[:, s], func=ACT.Exp)
 
-        a_sb = sb.tile([P, T], F32, name="a_sb")
+        a_sb = sb.tile([P, T], F32, name="a_sb", tag="a_then_den")
         for h in range(2):
             cols = slice(BANK * h, BANK * (h + 1))
             bank = ps.tile([P, BANK], F32, name="a_bank%d" % h, tag="bank%d" % (3 + h))
             score(bank[:], q_codes, q_scales, BANK * h, BANK)
             nc.vector.tensor_copy(out=a_sb[:, cols], in_=bank[:])
         a_lam = sb.tile([P, I], F32, name="a_lam")
-        a_picked = sb.tile([P, I], F32, name="a_picked", tag="picked_then_den")
+        a_picked = sb.tile([P, I], F32, name="a_picked")
         nc.vector.tensor_copy(a_picked[:], a_sb[:].indirect(list1[:]))
-        nc.vector.tensor_scalar(out=a_lam[:], in0=a_picked[:], scalar1=lam_sb[:], scalar2=None, op0=ALU.mult)
 
         root_e = math.exp(0.5)
         soft = sb.tile([P, I], F32, name="soft")
-        den = sb.tile([P, I], F32, name="den", tag="picked_then_den")
+        den = sb.tile([P, I], F32, name="den", tag="a_then_den")
         log_den = sb.tile([P, I], F32, name="log_den")
         inv = sb.tile([P, I], F32, name="inv")
         for s in (slice(SPLIT, I), slice(0, SPLIT)):
@@ -148,6 +147,7 @@ def tile_attend_worthfor_lean_twiceput_heads_kernel(
             nc.scalar.activation(out=log_den[:, s], in_=den[:, s], func=ACT.Ln)
         by_vector = slice(0, BY_VECTOR)
         by_scalar = slice(BY_VECTOR, I)
+        nc.vector.tensor_scalar(out=a_lam[:], in0=a_picked[:], scalar1=lam_sb[:], scalar2=None, op0=ALU.mult)
         nc.vector.reciprocal(out=inv[:, by_vector], in_=den[:, by_vector])
         nc.scalar.activation(out=inv[:, by_scalar], in_=log_den[:, by_scalar], func=ACT.Exp, scale=-1.0)
 

@@ -20,7 +20,6 @@ ACT = mybir.ActivationFunctionType
 P = 128
 PACK = 4
 BANK = 512
-B_PASS = 256
 B_PASSES = (256, 256, 256, 128, 128)
 PER_COLUMN = 16
 EXP_CAP = 40.0
@@ -54,7 +53,7 @@ def tile_attend_worthfor_lean_twiceput_heads_kernel(
         words = keys_words[0].rearrange("p n t -> p (n t)")
         k_words = []
         for h in range(2):
-            kw = sb.tile([P, BANK], U32, name="k_words%d" % h, tag="words%d" % h, align_bytes=64)
+            kw = sb.tile([P, BANK], U32, name="k_words%d" % h, align_bytes=64)
             nc.sync.dma_start(
                 out=kw[:].bitcast(I32),
                 in_=words[:, PACK * BANK * h : PACK * BANK * (h + 1)].bitcast(I32),
@@ -77,6 +76,9 @@ def tile_attend_worthfor_lean_twiceput_heads_kernel(
         f2 = sb.tile([P, T], F32, name="f2")
         nc.vector.memset(f1[:], 0.0)
         nc.vector.memset(f2[:], 0.0)
+
+        ident = sb.tile([P, P], F32, name="ident")
+        make_identity(nc, ident[:])
 
         def quantise(raw, name, cast):
             grouped = sb.tile([P, Q, PACK], BF16, name=name + "_bf", align_bytes=64)
@@ -114,16 +116,19 @@ def tile_attend_worthfor_lean_twiceput_heads_kernel(
             first = first + width
 
         x = sb.tile([P, I], F32, name="x")
-        x_cap = sb.tile([P, I], F32, name="x_cap")
+        x_cap = [
+            sb.tile([P, I // 2], F32, name="x_cap0", tag="capped_a_den"),
+            sb.tile([P, I // 2], F32, name="x_cap1"),
+        ]
         e = sb.tile([P, I], F32, name="e")
         halves = [slice(0, I // 2), slice(I // 2, I)]
         nc.vector.tensor_copy(x[:, halves[0]], b_sb[:].indirect(offsets(list2, halves[0])))
         nc.scalar.activation(x[:, halves[1]], b_sb[:].indirect(offsets(list2, halves[1])), ACT.Copy)
-        for s in halves:
-            nc.vector.tensor_scalar(out=x_cap[:, s], in0=x[:, s], scalar1=EXP_CAP, scalar2=None, op0=ALU.min)
-            nc.scalar.activation(out=e[:, s], in_=x_cap[:, s], func=ACT.Exp)
+        for capped, s in zip(x_cap, halves):
+            nc.vector.tensor_scalar(out=capped[:], in0=x[:, s], scalar1=EXP_CAP, scalar2=None, op0=ALU.min)
+            nc.scalar.activation(out=e[:, s], in_=capped[:], func=ACT.Exp)
 
-        a_sb = sb.tile([P, T], F32, name="a_sb", tag="a_then_den")
+        a_sb = sb.tile([P, T], F32, name="a_sb", tag="capped_a_den")
         for h in range(2):
             cols = slice(BANK * h, BANK * (h + 1))
             bank = ps.tile([P, BANK], F32, name="a_bank%d" % h, tag="bank%d" % (3 + h))
@@ -135,7 +140,7 @@ def tile_attend_worthfor_lean_twiceput_heads_kernel(
 
         root_e = math.exp(0.5)
         soft = sb.tile([P, I], F32, name="soft")
-        den = sb.tile([P, I], F32, name="den", tag="a_then_den")
+        den = sb.tile([P, I], F32, name="den", tag="capped_a_den")
         log_den = sb.tile([P, I], F32, name="log_den")
         inv = sb.tile([P, I], F32, name="inv")
         for s in (slice(SPLIT, I), slice(0, SPLIT)):
@@ -152,31 +157,26 @@ def tile_attend_worthfor_lean_twiceput_heads_kernel(
         nc.scalar.activation(out=inv[:, by_scalar], in_=log_den[:, by_scalar], func=ACT.Exp, scale=-1.0)
 
         blocks = BANK // P
-        ident = sb.tile([P, P], F32, name="ident", tag="words1", align_bytes=64)
-        make_identity(nc, ident[:])
-        quarters = T // B_PASS
-        pair = B_PASS // P
-        tags = ["bank0", "bank1", "bank2", "bank5"]
-        turned_banks = [ps.tile([P, pair, P], F32, name="turned%d" % n, tag=tags[n]) for n in range(quarters)]
-        for n in range(quarters):
-            for j in range(pair):
-                c = slice(B_PASS * n + P * j, B_PASS * n + P * (j + 1))
-                nc.tensor.matmul(turned_banks[n][:, j, :], old_sb[:, c], ident[:], start=(j == 0), stop=False, is_transpose=True)
+        turned_banks = [ps.tile([P, blocks, P], F32, name="turned%d" % h, tag="bank%d" % (3 + h)) for h in range(2)]
+        for h in range(2):
+            for j in range(blocks):
+                c = slice(BANK * h + P * j, BANK * h + P * (j + 1))
+                nc.tensor.matmul(turned_banks[h][:, j, :], old_sb[:, c], ident[:], start=(j == 0), stop=False, is_transpose=True)
 
         for s in (by_vector, by_scalar):
             nc.vector.tensor_tensor(f1[:].indirect(offsets(list1, s)), a_lam[:, s], inv[:, s], ALU.mult)
             nc.vector.tensor_tensor(f2[:].indirect(offsets(list3, s)), a_lam[:, s], inv[:, s], ALU.mult)
 
-        back = [ps.tile([P, BANK], F32, name="back%d" % h, tag="bank%d" % (3 + h)) for h in range(2)]
-        for n in range(quarters):
-            for j in range(pair):
-                c = slice(B_PASS * n + P * j, B_PASS * n + P * (j + 1))
-                nc.tensor.matmul(turned_banks[n][:, j, :], f1[:, c], ident[:], start=False, stop=(j == pair - 1), is_transpose=True)
-            turned = sb.tile([P, pair, P], F32, name="turned_sb%d" % n)
-            nc.scalar.copy(out=turned[:], in_=turned_banks[n][:])
-            for j in range(pair):
-                h, within = divmod(B_PASS * n + P * j, BANK)
-                nc.tensor.transpose(back[h][:, within : within + P], turned[:, j, :], ident[:])
+        for h in range(2):
+            for j in range(blocks):
+                c = slice(BANK * h + P * j, BANK * h + P * (j + 1))
+                nc.tensor.matmul(turned_banks[h][:, j, :], f1[:, c], ident[:], start=False, stop=(j == blocks - 1), is_transpose=True)
+        back = [ps.tile([P, BANK], F32, name="back%d" % h, tag="bank%d" % h) for h in range(2)]
+        for h in range(2):
+            turned = sb.tile([P, blocks, P], F32, name="turned_sb%d" % h)
+            nc.scalar.copy(out=turned[:], in_=turned_banks[h][:])
+            for j in range(blocks):
+                nc.tensor.transpose(back[h][:, P * j : P * (j + 1)], turned[:, j, :], ident[:])
         for h in range(2):
             cols = slice(BANK * h, BANK * (h + 1))
             result = sb.tile([P, BANK], F32, name="result%d" % h)

import math
from contextlib import ExitStack

import concourse.mybir as mybir
from concourse.masks import make_identity

D, T, I, Q = 512, 1024, 512, 128
FLOPS = 2 * 2 * D * Q * T

F32 = mybir.dt.float32
BF16 = mybir.dt.bfloat16
I32 = mybir.dt.int32
U32 = mybir.dt.uint32
U16 = mybir.dt.uint16
U8 = mybir.dt.uint8
FP8X4 = mybir.dt.float8_e4m3fn_x4
ALU = mybir.AluOpType
ACT = mybir.ActivationFunctionType

P = 128
PACK = 4
BANK = 512
B_PASSES = (256, 256, 256, 128, 128)
PER_COLUMN = 16
EXP_CAP = 40.0
SPLIT = 320
BY_VECTOR = 128


def offsets(lists, slots):
    return lists[:, slots.start // PER_COLUMN : slots.stop // PER_COLUMN]


def tile_attend_worthfor_lean_twiceput_heads_kernel(
    tc, query, query2, keys_words, keys_scales, lam, old, share2, offs, offs2, offs3, out
):
    nc = tc.nc
    with ExitStack() as ctx:
        sb = ctx.enter_context(tc.tile_pool(name="sb", bufs=1))
        ps = ctx.enter_context(tc.psum_pool(name="ps", bufs=1))

        k_scale = sb.tile([P, T], U8, name="k_scale", align_bytes=64)
        nc.gpsimd.memset(k_scale[:].bitcast(I32), 0)
        q2_raw = sb.tile([P, PACK, Q], F32, name="q2_raw")
        nc.sync.dma_start(out=q2_raw[:], in_=query2.rearrange("(p j) q -> p j q", j=PACK))
        q_raw = sb.tile([P, PACK, Q], F32, name="q_raw")
        nc.sync.dma_start(out=q_raw[:], in_=query.rearrange("(p j) q -> p j q", j=PACK))
        for quad in range(4):
            nc.sync.dma_start(
                out=k_scale[32 * quad : 32 * quad + 4, :].bitcast(I32),
                in_=keys_scales[0, 4 * quad : 4 * quad + 4, :].bitcast(I32),
            )
        words = keys_words[0].rearrange("p n t -> p (n t)")
        k_words = []
        for h in range(2):
            kw = sb.tile([P, BANK], U32, name="k_words%d" % h, align_bytes=64)
            nc.sync.dma_start(
                out=kw[:].bitcast(I32),
                in_=words[:, PACK * BANK * h : PACK * BANK * (h + 1)].bitcast(I32),
            )
            k_words.append(kw)
        list2 = sb.tile([P, I // PER_COLUMN], U16, name="list2")
        nc.sync.dma_start(list2[:], offs2)
        list1 = sb.tile([P, I // PER_COLUMN], U16, name="list1")
        nc.sync.dma_start(list1[:], offs)
        lam_sb = sb.tile([P, 1], F32, name="lam_sb")
        nc.sync.dma_start(out=lam_sb[:], in_=lam)
        list3 = sb.tile([P, I // PER_COLUMN], U16, name="list3")
        nc.sync.dma_start(list3[:], offs3)
        old_sb = sb.tile([P, T], F32, name="old_sb")
        nc.sync.dma_start(out=old_sb[:], in_=old)
        share_sb = sb.tile([P, 1], F32, name="share_sb")
        nc.sync.dma_start(out=share_sb[:], in_=share2)

        f1 = sb.tile([P, T], F32, name="f1")
        f2 = sb.tile([P, T], F32, name="f2")
        nc.vector.memset(f1[:], 0.0)
        nc.vector.memset(f2[:], 0.0)

        ident = sb.tile([P, P], F32, name="ident")
        make_identity(nc, ident[:])

        def quantise(raw, name, cast):
            grouped = sb.tile([P, Q, PACK], BF16, name=name + "_bf", align_bytes=64)
            cast(out=grouped[:], in_=raw[:].rearrange("p j q -> p q j"))
            codes = sb.tile([P, Q], U32, name=name + "_codes", align_bytes=64)
            scales = sb.tile([P, Q], U8, name=name + "_scales", align_bytes=64)
            nc.vector.quantize_mx(
                out=codes[:].bitcast(FP8X4),
                scales=scales[:],
                in_=grouped[:].rearrange("p q j -> p (q j)"),
            )
            return codes, scales

        def score(bank, codes, scales, first, width):
            h, within = divmod(first, BANK)
            nc.tensor.matmul_mx(
                out=bank,
                lhsT=codes[:].bitcast(FP8X4),
                lhsT_scale=scales[:],
                rhs=k_words[h][:, within : within + width].bitcast(FP8X4),
                rhs_scale=k_scale[:, first : first + width],
                start=True,
                stop=True,
            )

        q2_codes, q2_scales = quantise(q2_raw, "q2", nc.vector.tensor_copy)
        q_codes, q_scales = quantise(q_raw, "q", nc.scalar.copy)
        b_sb = sb.tile([P, T], F32, name="b_sb")
        first = 0
        for n, width in enumerate(B_PASSES):
            bank = ps.tile([P, width], F32, name="b_bank%d" % n, tag="bank%d" % n)
            score(bank[:], q2_codes, q2_scales, first, width)
            copy_out = nc.vector.tensor_copy if n % 2 == 0 else nc.scalar.copy
            copy_out(out=b_sb[:, first : first + width], in_=bank[:])
            first = first + width

        x = sb.tile([P, I], F32, name="x")
        x_cap = [
            sb.tile([P, I // 2], F32, name="x_cap0", tag="capped_a_den"),
            sb.tile([P, I // 2], F32, name="x_cap1"),
        ]
        e = sb.tile([P, I], F32, name="e")
        halves = [slice(0, I // 2), slice(I // 2, I)]
        nc.vector.tensor_copy(x[:, halves[0]], b_sb[:].indirect(offsets(list2, halves[0])))
        nc.scalar.activation(x[:, halves[1]], b_sb[:].indirect(offsets(list2, halves[1])), ACT.Copy)
        for capped, s in zip(x_cap, halves):
            nc.vector.tensor_scalar(out=capped[:], in0=x[:, s], scalar1=EXP_CAP, scalar2=None, op0=ALU.min)
            nc.scalar.activation(out=e[:, s], in_=capped[:], func=ACT.Exp)

        a_sb = sb.tile([P, T], F32, name="a_sb", tag="capped_a_den")
        for h in range(2):
            cols = slice(BANK * h, BANK * (h + 1))
            bank = ps.tile([P, BANK], F32, name="a_bank%d" % h, tag="bank%d" % (3 + h))
            score(bank[:], q_codes, q_scales, BANK * h, BANK)
            nc.vector.tensor_copy(out=a_sb[:, cols], in_=bank[:])
        a_lam = sb.tile([P, I], F32, name="a_lam")
        a_picked = sb.tile([P, I], F32, name="a_picked")
        nc.vector.tensor_copy(a_picked[:], a_sb[:].indirect(list1[:]))

        root_e = math.exp(0.5)
        soft = sb.tile([P, I], F32, name="soft")
        den = sb.tile([P, I], F32, name="den", tag="capped_a_den")
        log_den = sb.tile([P, I], F32, name="log_den")
        inv = sb.tile([P, I], F32, name="inv")
        for s in (slice(SPLIT, I), slice(0, SPLIT)):
            nc.scalar.activation(out=soft[:, s], in_=e[:, s], func=ACT.Ln, scale=root_e, bias=root_e)
            nc.vector.scalar_tensor_tensor(
                out=den[:, s], in0=x[:, s], scalar=0.5, in1=soft[:, s], op0=ALU.add, op1=ALU.max
            )
        for s in (slice(SPLIT, I), slice(BY_VECTOR, SPLIT)):
            nc.scalar.activation(out=log_den[:, s], in_=den[:, s], func=ACT.Ln)
        by_vector = slice(0, BY_VECTOR)
        by_scalar = slice(BY_VECTOR, I)
        nc.vector.tensor_scalar(out=a_lam[:], in0=a_picked[:], scalar1=lam_sb[:], scalar2=None, op0=ALU.mult)
        nc.vector.reciprocal(out=inv[:, by_vector], in_=den[:, by_vector])
        nc.scalar.activation(out=inv[:, by_scalar], in_=log_den[:, by_scalar], func=ACT.Exp, scale=-1.0)

        blocks = BANK // P
        turned_banks = [ps.tile([P, blocks, P], F32, name="turned%d" % h, tag="bank%d" % (3 + h)) for h in range(2)]
        for h in range(2):
            for j in range(blocks):
                c = slice(BANK * h + P * j, BANK * h + P * (j + 1))
                nc.tensor.matmul(turned_banks[h][:, j, :], old_sb[:, c], ident[:], start=(j == 0), stop=False, is_transpose=True)

        for s in (by_vector, by_scalar):
            nc.vector.tensor_tensor(f1[:].indirect(offsets(list1, s)), a_lam[:, s], inv[:, s], ALU.mult)
            nc.vector.tensor_tensor(f2[:].indirect(offsets(list3, s)), a_lam[:, s], inv[:, s], ALU.mult)

        for h in range(2):
            for j in range(blocks):
                c = slice(BANK * h + P * j, BANK * h + P * (j + 1))
                nc.tensor.matmul(turned_banks[h][:, j, :], f1[:, c], ident[:], start=False, stop=(j == blocks - 1), is_transpose=True)
        back = [ps.tile([P, BANK], F32, name="back%d" % h, tag="bank%d" % h) for h in range(2)]
        for h in range(2):
            turned = sb.tile([P, blocks, P], F32, name="turned_sb%d" % h)
            nc.scalar.copy(out=turned[:], in_=turned_banks[h][:])
            for j in range(blocks):
                nc.tensor.transpose(back[h][:, P * j : P * (j + 1)], turned[:, j, :], ident[:])
        for h in range(2):
            cols = slice(BANK * h, BANK * (h + 1))
            result = sb.tile([P, BANK], F32, name="result%d" % h)
            nc.vector.scalar_tensor_tensor(
                out=result[:],
                in0=f2[:, cols],
                scalar=share_sb[:],
                in1=back[h][:],
                op0=ALU.mult,
                op1=ALU.add,
            )
            queue = nc.sync if h == 0 else nc.scalar
            queue.dma_start(out=out[:, cols], in_=result[:])
